import numpy as np
import ml_dtypes


def mxq(x, axis, fmt="e4m3"):
    dtype, down = {"e4m3": (ml_dtypes.float8_e4m3fn, 7), "e5m2": (ml_dtypes.float8_e5m2, 14)}[fmt]
    v = np.moveaxis(np.asarray(x, np.float32).astype(ml_dtypes.bfloat16).astype(np.float64), axis, -1)
    blocks = v.reshape(v.shape[:-1] + (-1, 32))
    amax = np.abs(blocks).max(-1, keepdims=True)
    byte = np.maximum(np.where(amax > 0, np.frexp(amax)[1] - 1 + 127, 0) - down, 1)
    scale = np.exp2(byte - 127.0)
    codes = (blocks / scale).astype(np.float32).astype(dtype).astype(np.float64)
    return np.moveaxis((codes * scale).reshape(v.shape), -1, axis)


WIDE = False


def mx_kscale(k):
    if not WIDE:
        return np.ones(k)
    levels = np.array([10, -10, 5, -5, 0])
    if k % 512:
        return np.exp2(np.random.permutation(np.resize(levels, k // 32))).repeat(32)
    a = np.empty((k // 512, 16))
    for p in range(k // 512):
        a[p, :8] = np.random.permutation(np.resize(levels, 8))
        for g in range(8):
            far = levels[np.abs(levels - a[p, g]) >= 10]
            a[p, g + 8] = far[np.random.randint(len(far))]
    return np.exp2(a.ravel()).repeat(32)


def f64(x):
    return np.asarray(x).astype(np.float64)


def striped(idx):
    return np.tile(idx.reshape(-1, 16).T, (8, 1)).astype(np.uint16)


def unstriped(offs):
    return offs[:16].T.reshape(-1).astype(np.int64)


def striped8(idx):
    return np.concatenate([x.reshape(-1, 16).T for x in idx]).astype(np.uint16)


def runs(offs, k):
    lists = np.stack([offs[16 * r : 16 * r + 16].T.reshape(-1) for r in range(8)]).astype(np.int64)
    return lists[np.arange(k) % 512 // 64]


def pack_weight(w):
    k, n = w.shape
    w = f64(np.asarray(w, np.float32).astype(ml_dtypes.bfloat16)).reshape(k // 32, 32, n)
    amax = np.abs(w).max(1)
    byte = np.clip(np.where(amax > 0, np.frexp(amax)[1] - 1 + 127 - 7, 1), 1, 254)
    scaled = (w * np.exp2(127.0 - byte)[:, None, :]).reshape(k, n).astype(np.float32)
    words = np.ascontiguousarray(scaled.reshape(k // 512, 128, 4, n).transpose(0, 1, 3, 2)).astype(ml_dtypes.float8_e4m3fn).view(np.uint8)
    return words, np.ascontiguousarray(byte.astype(np.uint8).reshape(k // 512, 16, n))


def unpack_weight(words, scales):
    g, p, n, _ = words.shape
    vals = np.ascontiguousarray(words).view(ml_dtypes.float8_e4m3fn).astype(np.float64) * np.repeat(np.exp2(scales.astype(np.float64) - 127.0), 8, axis=1)[..., None]
    return vals.transpose(0, 1, 3, 2).reshape(g * 512, n)


K, T, S, V, N, H = 512, 2048, 512, 256, 512, 512


def setup_inputs():
    n = np.random.standard_normal
    s = mx_kscale(K)[:, None]
    u = mx_kscale(H)
    packed_xT = pack_weight(n((K, T)) * s)
    perm = np.stack([np.random.permutation(S) for _ in range(8)])
    return {
        "x_words": packed_xT[0],
        "x_scales": packed_xT[1],
        "w1": (n((K, H)) / np.sqrt(K) / s * u).astype(np.float32),
        "w2": (n((H, H)) / np.sqrt(H) / u[:, None] * u).astype(np.float32),
        "res": (2 * n((N, S))).astype(np.float32),
        "w3": (n((H, N)) / np.sqrt(H) / u[:, None]).astype(np.float32),
        "offs": striped(np.random.permutation(T)[:S]),
        "la": striped8(perm[:, :V]),
        "lb": striped8(perm[:, V:]),
        "mate": striped8(np.stack([np.random.permutation(S) for _ in range(8)])),
    }


def reference(x_words, x_scales, w1, w2, res, w3, offs, la, lb, mate):
    xq = unpack_weight(x_words, x_scales)[:, unstriped(offs)]
    y = mxq(f64(w1), 0, "e4m3").T @ xq
    a = y[np.arange(H)[:, None], runs(la, H)]
    b = y[np.arange(H)[:, None], runs(lb, H)]
    df = a - b
    sm = a + b
    p = np.zeros((H, S))
    p[np.arange(H)[:, None], runs(la, H)] = sm
    z = p.copy()
    z[np.arange(H)[:, None], runs(lb, H)] = df
    h = mxq(f64(w2), 0, "e4m3").T @ mxq(z, 0, "e4m3")
    z2 = h - (h[np.arange(H)[:, None], runs(mate, H)])
    return f64(res) + 0.5 * ((mxq(f64(w3), 0, "e4m3").T @ mxq(z2, 0, "e4m3")))

@@ -1,0 +1,234 @@
+from contextlib import ExitStack
+
+import concourse.mybir as mybir
+
+F32 = mybir.dt.float32
+BF16 = mybir.dt.bfloat16
+I32 = mybir.dt.int32
+U32 = mybir.dt.uint32
+U16 = mybir.dt.uint16
+U8 = mybir.dt.uint8
+FP8X4 = mybir.dt.float8_e4m3fn_x4
+ADD = mybir.AluOpType.add
+MULT = mybir.AluOpType.mult
+COPY = mybir.ActivationFunctionType.Copy
+
+P = 128
+PACK = 4
+T = 2048
+S = 512
+V = 256
+HALF = 256
+CHUNK = 128
+FLOPS = 3 * 2 * 512 * 512 * 512
+
+
+def tile_picked_crossfft_none_p_kernel(
+    tc, x_words, x_scales, w1, w2, res, w3, offs, la, lb, mate, out
+):
+    nc = tc.nc
+    with ExitStack() as ctx:
+        lists = ctx.enter_context(tc.tile_pool(name="lists", bufs=1))
+        keep = ctx.enter_context(tc.tile_pool(name="keep", bufs=1))
+        windows = ctx.enter_context(tc.tile_pool(name="windows", bufs=1))
+        psum = ctx.enter_context(tc.psum_pool(name="psum", bufs=8))
+
+        def entries(tile, first, count):
+            return tile[:, first // 16 : (first + count) // 16]
+
+        def quantize(codes, scales, grouped):
+            nc.vector.quantize_mx(out=codes.bitcast(FP8X4), scales=scales, in_=grouped)
+
+        def product(acc, w_codes, w_scales, t, codes, scales):
+            cols = slice(t * P, (t + 1) * P)
+            nc.tensor.matmul_mx(
+                out=acc, lhsT=w_codes[:, cols].bitcast(FP8X4), lhsT_scale=w_scales[:, cols],
+                rhs=codes.bitcast(FP8X4), rhs_scale=scales, start=True, stop=True,
+            )
+
+        def dealt_views(grouped, raw, m0, m1):
+            dst = grouped[:].rearrange("p (t m j) -> p m j t", t=PACK, j=PACK)[:, m0:m1]
+            src = raw[:].rearrange("p j (m t) -> p m j t", t=PACK)[:, m0:m1]
+            return dst, src
+
+        xs_table = keep.tile([P, T], U8, name="xs_table")
+        nc.vector.memset(xs_table[:].bitcast(I32), 0)
+        offs_t = lists.tile([P, S // 16], U16, name="offs_t")
+        nc.sync.dma_start(offs_t[:], offs)
+        xs_rows = keep.tile([P, T], U8, name="xs_rows")
+        for q in range(4):
+            rows = slice(32 * q, 32 * q + 4)
+            nc.sync.dma_start(xs_rows[rows, :].bitcast(I32), x_scales[0, 4 * q : 4 * q + 4, :].bitcast(I32))
+            nc.vector.tensor_copy(xs_table[rows, :].bitcast(I32), xs_rows[rows, :].bitcast(I32))
+        w1_raw = keep.tile([P, PACK, S], F32, name="w1_raw", tag="raw")
+        nc.sync.dma_start(w1_raw[:], w1.rearrange("(p j) c -> p j c", j=PACK))
+        xw_table = keep.tile([P, T], U32, name="xw_table")
+        nc.sync.dma_start(xw_table[:].bitcast(I32), x_words[0].rearrange("p n t -> p (n t)").bitcast(I32))
+        la_t = lists.tile([P, V // 16], U16, name="la_t")
+        nc.sync.dma_start(la_t[:], la)
+        lb_t = lists.tile([P, V // 16], U16, name="lb_t")
+        nc.sync.dma_start(lb_t[:], lb)
+        mate_t = lists.tile([P, S // 16], U16, name="mate_t")
+        nc.sync.dma_start(mate_t[:], mate)
+
+        x_sc = keep.tile([P, S], U8, name="x_sc", align_bytes=64)
+        nc.vector.tensor_copy(x_sc[:], xs_table[:].indirect(offs_t[:]))
+
+        w1_codes = keep.tile([P, S], U32, name="w1_codes", align_bytes=64)
+        w1_scales = keep.tile([P, S], U8, name="w1_scales", align_bytes=64)
+        for n, odd in enumerate((1, 0)):
+            grouped = keep.tile(
+                [P, 2 * P * PACK], BF16, name="w1_grouped%d" % odd, tag=("w1g_even", "w1g_w3raw")[odd], align_bytes=64
+            )
+            dst = grouped[:].rearrange("p (u m j) -> p m j u", u=2, j=PACK)
+            src = w1_raw[:].rearrange("p j (m u v) -> p m j u v", u=2, v=2)[:, :, :, :, odd]
+            if odd:
+                nc.vector.tensor_copy(dst, src)
+            else:
+                nc.scalar.copy(dst, src)
+            cols = slice(n * HALF, (n + 1) * HALF)
+            quantize(w1_codes[:, cols], w1_scales[:, cols], grouped[:])
+
+        w2_raw = keep.tile([P, PACK, S], F32, name="w2_raw", tag="raw")
+        nc.sync.dma_start(w2_raw[:], w2.rearrange("(p j) c -> p j c", j=PACK))
+        w3_raw = keep.tile([P, PACK, S], F32, name="w3_raw", tag="w1g_w3raw", align_bytes=64)
+        nc.sync.dma_start(w3_raw[:], w3.rearrange("(p j) c -> p j c", j=PACK))
+
+        x_codes = keep.tile([P, S], U32, name="x_codes", align_bytes=64)
+        for h in range(2):
+            cols = slice(h * HALF, (h + 1) * HALF)
+            nc.vector.tensor_copy(x_codes[:, cols], xw_table[:].indirect(entries(offs_t, h * HALF, HALF)))
+
+        order = (1, 3, 0, 2)
+        row_bytes = S * 4
+        y = {}
+        for n, t in enumerate(order):
+            y[t] = windows.tile([P, S], F32, name="y%d" % t, offset=n * row_bytes)
+            pieces = 2 if n == 0 else 1
+            width = S // pieces
+            for h in range(pieces):
+                cols = slice(h * width, (h + 1) * width)
+                acc = psum.tile([P, width], F32, name="acc", tag="bank")
+                product(acc[:], w1_codes, w1_scales, n, x_codes[:, cols], x_sc[:, cols])
+                nc.scalar.copy(y[t][:, cols], acc[:])
+
+        a, b, nb = {}, {}, {}
+        for t in order:
+            a[t] = keep.tile([P, V], F32, name="a%d" % t)
+            b[t] = keep.tile([P, V], F32, name="b%d" % t)
+            nb[t] = keep.tile([P, V], F32, name="nb%d" % t)
+            nc.vector.tensor_copy(a[t][:], y[t][:].indirect(la_t[:]))
+            nc.vector.tensor_copy(b[t][:], y[t][:].indirect(lb_t[:]))
+            nc.scalar.activation(nb[t][:], b[t][:], COPY, scale=-1.0)
+
+        w2_grouped = keep.tile([P, PACK * S], BF16, name="w2_grouped", align_bytes=64)
+        for h in range(2):
+            dst, src = dealt_views(w2_grouped, w2_raw, h * 64, (h + 1) * 64)
+            nc.scalar.copy(dst, src)
+        res_t = keep.tile([P, PACK, S], F32, name="res_t", tag="raw")
+        nc.sync.dma_start(res_t[:], res.rearrange("(t p) j -> p t j", p=P))
+
+        def scatter_pair(window, planes):
+            for t in planes:
+                nc.vector.tensor_tensor(window[t][:].indirect(la_t[:]), a[t][:], b[t][:], ADD)
+            for t in planes:
+                nc.vector.tensor_tensor(window[t][:].indirect(lb_t[:]), a[t][:], nb[t][:], ADD)
+
+        z_odd = {
+            1: windows.tile([P, S], F32, name="z1", offset=5 * row_bytes // 2),
+            3: windows.tile([P, S], F32, name="z3", offset=7 * row_bytes // 2),
+        }
+        scatter_pair(z_odd, (1, 3))
+        z_pair = {}
+        for t in (0, 2):
+            z_pair[t] = keep.tile([P, 2 * S], F32, name="z_pair%d" % t)
+            nc.scalar.copy(z_pair[t][:, S:], z_odd[t + 1][:])
+
+        w2_codes = keep.tile([P, S], U32, name="w2_codes", align_bytes=64)
+        w2_scales = keep.tile([P, S], U8, name="w2_scales", align_bytes=64)
+        quantize(w2_codes[:], w2_scales[:], w2_grouped[:])
+
+        w3_grouped = keep.tile([P, PACK * S], BF16, name="w3_grouped", align_bytes=64)
+        nc.scalar.copy(
+            w3_grouped[:].rearrange("p (c i j) -> p c j i", i=4, j=PACK),
+            w3_raw[:].rearrange("p j (c i) -> p c j i", i=4),
+        )
+
+        scatter_pair(z_pair, (0, 2))
+
+        z_grouped = [
+            keep.tile([P, HALF, PACK], BF16, name="z_grouped%d" % h, tag="zg%d" % h, align_bytes=64) for h in range(2)
+        ]
+
+        def pair_views(t, c0, c1):
+            h = c0 // HALF
+            dst = z_grouped[h][:, c0 - h * HALF : c1 - h * HALF, t : t + 2]
+            src = z_pair[t][:].rearrange("p (s j) -> p j s", s=2)[:, c0:c1, :]
+            return dst, src
+
+        for h in range(2):
+            dst, src = pair_views(0, h * HALF, (h + 1) * HALF)
+            nc.scalar.copy(dst, src)
+        for c0, c1 in ((0, HALF), (HALF, HALF + CHUNK)):
+            dst, src = pair_views(2, c0, c1)
+            nc.vector.tensor_copy(dst, src)
+        dst, src = pair_views(2, HALF + CHUNK, S)
+        nc.scalar.copy(dst, src)
+
+        z_codes = keep.tile([P, S], U32, name="z_codes", align_bytes=64)
+        z_scales = keep.tile([P, S], U8, name="z_scales", align_bytes=64)
+        for h in range(2):
+            cols = slice(h * HALF, (h + 1) * HALF)
+            quantize(z_codes[:, cols], z_scales[:, cols], z_grouped[h][:].rearrange("p c t -> p (c t)"))
+        w3_codes = keep.tile([P, S], U32, name="w3_codes", tag="zg0", align_bytes=64)
+        w3_scales = keep.tile([P, S], U8, name="w3_scales", align_bytes=64)
+        quantize(w3_codes[:], w3_scales[:], w3_grouped[:])
+
+        neg_h = [keep.tile([P, S], F32, name="neg_h%d" % t) for t in range(PACK)]
+        h_plain = keep.tile([P, PACK, S], F32, name="h_plain")
+        z2 = keep.tile([P, PACK, S], F32, name="z2")
+
+        def subtract_mate(t, c0, width):
+            cols = slice(c0, c0 + width)
+            nc.vector.tensor_tensor(
+                z2[:, t, cols], neg_h[t][:].indirect(entries(mate_t, c0, width)), h_plain[:, t, cols], ADD
+            )
+
+        for h in range(2):
+            cols = slice(h * HALF, (h + 1) * HALF)
+            acc = psum.tile([P, HALF], F32, name="acc", tag="bank")
+            product(acc[:], w2_codes, w2_scales, 0, z_codes[:, cols], z_scales[:, cols])
+            nc.scalar.activation(neg_h[0][:, cols], acc[:], COPY, scale=-1.0)
+            nc.scalar.copy(h_plain[:, 0, cols], acc[:])
+        for h in range(2):
+            subtract_mate(0, h * HALF, HALF)
+        h_acc = {}
+        for t in range(1, PACK):
+            h_acc[t] = psum.tile([P, S], F32, name="acc", tag="bank")
+            product(h_acc[t][:], w2_codes, w2_scales, t, z_codes[:], z_scales[:])
+            nc.scalar.activation(neg_h[t][:], h_acc[t][:], COPY, scale=-1.0)
+            if t == 1:
+                nc.scalar.copy(h_plain[:, 1, :], h_acc[1][:])
+                for h in range(2):
+                    subtract_mate(1, h * HALF, HALF)
+
+        out_view = out.rearrange("(t p) j -> p t j", p=P)
+        for c in range(S // CHUNK):
+            cols = slice(c * CHUNK, (c + 1) * CHUNK)
+            for t in (2, 3):
+                nc.scalar.copy(h_plain[:, t, cols], h_acc[t][:, cols])
+                subtract_mate(t, c * CHUNK, CHUNK)
+            z2_grouped = keep.tile([P, CHUNK * PACK], BF16, name="z2_grouped%d" % c, align_bytes=64)
+            nc.scalar.copy(
+                z2_grouped[:].rearrange("p (c i t) -> p c t i", i=4, t=PACK),
+                z2[:, :, cols].rearrange("p t (c i) -> p c t i", i=4),
+            )
+            z2_codes = keep.tile([P, CHUNK], U32, name="z2_codes%d" % c, align_bytes=64)
+            z2_scales = keep.tile([P, CHUNK], U8, name="z2_scales%d" % c, align_bytes=64)
+            quantize(z2_codes[:], z2_scales[:], z2_grouped[:])
+            acc = psum.tile([P, PACK, CHUNK], F32, name="acc", tag="bank")
+            for t in range(PACK):
+                product(acc[:, t, :], w3_codes, w3_scales, t, z2_codes[:], z2_scales[:])
+            result = keep.tile([P, PACK, CHUNK], F32, name="result%d" % c)
+            nc.vector.scalar_tensor_tensor(result[:], acc[:], 0.5, res_t[:, :, cols], MULT, ADD)
+            nc.sync.dma_start(out_view[:, :, cols], result[:])

@@ -58,7 +58,7 @@ def tile_picked_crossfft_none_p_kernel(
         xs_rows = keep.tile([P, T], U8, name="xs_rows")
         for q in range(4):
             rows = slice(32 * q, 32 * q + 4)
-            nc.sync.dma_start(xs_rows[rows, :].bitcast(I32), x_scales[0, 4 * q : 4 * q + 4, :].bitcast(I32))
+            (nc.scalar if q < 2 else nc.sync).dma_start(xs_rows[rows, :].bitcast(I32), x_scales[0, 4 * q : 4 * q + 4, :].bitcast(I32))
             nc.vector.tensor_copy(xs_table[rows, :].bitcast(I32), xs_rows[rows, :].bitcast(I32))
         w1_raw = keep.tile([P, PACK, S], F32, name="w1_raw", tag="raw")
         nc.sync.dma_start(w1_raw[:], w1.rearrange("(p j) c -> p j c", j=PACK))
@@ -177,14 +177,16 @@ def tile_picked_crossfft_none_p_kernel(
 
         z_codes = keep.tile([P, S], U32, name="z_codes", align_bytes=64)
         z_scales = keep.tile([P, S], U8, name="z_scales", align_bytes=64)
-        for h in range(2):
-            cols = slice(h * HALF, (h + 1) * HALF)
-            quantize(z_codes[:, cols], z_scales[:, cols], z_grouped[h][:].rearrange("p c t -> p (c t)"))
+        z_pieces = ((0, HALF), (HALF, HALF + CHUNK), (HALF + CHUNK, S))
+        for c0, c1 in z_pieces:
+            h = c0 // HALF
+            grouped = z_grouped[h][:, c0 - h * HALF : c1 - h * HALF, :].rearrange("p c t -> p (c t)")
+            quantize(z_codes[:, c0:c1], z_scales[:, c0:c1], grouped)
         w3_codes = keep.tile([P, S], U32, name="w3_codes", tag="zg0", align_bytes=64)
         w3_scales = keep.tile([P, S], U8, name="w3_scales", align_bytes=64)
         quantize(w3_codes[:], w3_scales[:], w3_grouped[:])
 
-        neg_h = [keep.tile([P, S], F32, name="neg_h%d" % t) for t in range(PACK)]
+        neg_h = [keep.tile([P, S], F32, name="neg_h%d" % t, tag="neg_h%d" % t, align_bytes=64) for t in range(PACK)]
         h_plain = keep.tile([P, PACK, S], F32, name="h_plain")
         z2 = keep.tile([P, PACK, S], F32, name="z2")
 
@@ -194,12 +196,18 @@ def tile_picked_crossfft_none_p_kernel(
                 z2[:, t, cols], neg_h[t][:].indirect(entries(mate_t, c0, width)), h_plain[:, t, cols], ADD
             )
 
-        for h in range(2):
-            cols = slice(h * HALF, (h + 1) * HALF)
-            acc = psum.tile([P, HALF], F32, name="acc", tag="bank")
+        first = []
+        for c0, c1 in z_pieces:
+            cols = slice(c0, c1)
+            acc = psum.tile([P, c1 - c0], F32, name="acc", tag="bank")
             product(acc[:], w2_codes, w2_scales, 0, z_codes[:, cols], z_scales[:, cols])
             nc.scalar.activation(neg_h[0][:, cols], acc[:], COPY, scale=-1.0)
-            nc.scalar.copy(h_plain[:, 0, cols], acc[:])
+            first.append((cols, acc))
+        for n, (cols, acc) in enumerate(first):
+            if n < 2:
+                nc.vector.tensor_copy(h_plain[:, 0, cols], acc[:])
+            else:
+                nc.scalar.copy(h_plain[:, 0, cols], acc[:])
         for h in range(2):
             subtract_mate(0, h * HALF, HALF)
         h_acc = {}
@@ -211,14 +219,20 @@ def tile_picked_crossfft_none_p_kernel(
                 nc.scalar.copy(h_plain[:, 1, :], h_acc[1][:])
                 for h in range(2):
                     subtract_mate(1, h * HALF, HALF)
+            else:
+                nc.scalar.copy(h_plain[:, t, :HALF], h_acc[t][:, :HALF])
+                subtract_mate(t, 0, HALF)
+        for t in (2, 3):
+            nc.scalar.copy(h_plain[:, t, HALF:], h_acc[t][:, HALF:])
+        subtract_mate(2, HALF, HALF)
+        for c0 in (HALF, HALF + CHUNK):
+            subtract_mate(3, c0, CHUNK)
 
         out_view = out.rearrange("(t p) j -> p t j", p=P)
+        finals = []
         for c in range(S // CHUNK):
             cols = slice(c * CHUNK, (c + 1) * CHUNK)
-            for t in (2, 3):
-                nc.scalar.copy(h_plain[:, t, cols], h_acc[t][:, cols])
-                subtract_mate(t, c * CHUNK, CHUNK)
-            z2_grouped = keep.tile([P, CHUNK * PACK], BF16, name="z2_grouped%d" % c, align_bytes=64)
+            z2_grouped = keep.tile([P, CHUNK * PACK], BF16, name="z2_grouped", tag="z2_grouped%d" % c, align_bytes=64)
             nc.scalar.copy(
                 z2_grouped[:].rearrange("p (c i t) -> p c t i", i=4, t=PACK),
                 z2[:, :, cols].rearrange("p t (c i) -> p c t i", i=4),
@@ -226,9 +240,15 @@ def tile_picked_crossfft_none_p_kernel(
             z2_codes = keep.tile([P, CHUNK], U32, name="z2_codes%d" % c, align_bytes=64)
             z2_scales = keep.tile([P, CHUNK], U8, name="z2_scales%d" % c, align_bytes=64)
             quantize(z2_codes[:], z2_scales[:], z2_grouped[:])
-            acc = psum.tile([P, PACK, CHUNK], F32, name="acc", tag="bank")
-            for t in range(PACK):
-                product(acc[:, t, :], w3_codes, w3_scales, t, z2_codes[:], z2_scales[:])
-            result = keep.tile([P, PACK, CHUNK], F32, name="result%d" % c)
-            nc.vector.scalar_tensor_tensor(result[:], acc[:], 0.5, res_t[:, :, cols], MULT, ADD)
-            nc.sync.dma_start(out_view[:, :, cols], result[:])
+            pieces = 2 if c == S // CHUNK - 1 else 1
+            rows = PACK // pieces
+            for n in range(pieces):
+                acc = psum.tile([P, rows, CHUNK], F32, name="acc", tag="bank")
+                for t in range(rows):
+                    product(acc[:, t, :], w3_codes, w3_scales, n * rows + t, z2_codes[:], z2_scales[:])
+                finals.append((acc, slice(n * rows, (n + 1) * rows), cols))
+        for n, (acc, rows, cols) in enumerate(finals):
+            tag = ("neg_h2", "neg_h3", "z2_grouped3", "neg_h0", "neg_h1")[n]
+            result = keep.tile([P, rows.stop - rows.start, CHUNK], F32, name="result", tag=tag, align_bytes=64)
+            nc.vector.scalar_tensor_tensor(result[:], acc[:], 0.5, res_t[:, rows, cols], MULT, ADD)
+            (nc.scalar if n == len(finals) - 1 else nc.sync).dma_start(out_view[:, rows, cols], result[:])

@@ -74,25 +74,24 @@ def tile_picked_crossfft_none_p_kernel(
         x_sc = keep.tile([P, S], U8, name="x_sc", align_bytes=64)
         nc.vector.tensor_copy(x_sc[:], xs_table[:].indirect(offs_t[:]))
 
+        def deal(engine_copy, raw, odd, name, tag):
+            grouped = keep.tile([P, 2 * P * PACK], BF16, name=name, tag=tag, align_bytes=64)
+            dst = grouped[:].rearrange("p (u m j) -> p m j u", u=2, j=PACK)
+            src = raw[:].rearrange("p j (m u v) -> p m j u v", u=2, v=2)[:, :, :, :, odd]
+            engine_copy(dst, src)
+            return grouped
+
         w1_codes = keep.tile([P, S], U32, name="w1_codes", align_bytes=64)
         w1_scales = keep.tile([P, S], U8, name="w1_scales", align_bytes=64)
-        for n, odd in enumerate((1, 0)):
-            grouped = keep.tile(
-                [P, 2 * P * PACK], BF16, name="w1_grouped%d" % odd, tag=("w1g_even", "w1g_w3raw")[odd], align_bytes=64
-            )
-            dst = grouped[:].rearrange("p (u m j) -> p m j u", u=2, j=PACK)
-            src = w1_raw[:].rearrange("p j (m u v) -> p m j u v", u=2, v=2)[:, :, :, :, odd]
-            if odd:
-                nc.vector.tensor_copy(dst, src)
-            else:
-                nc.scalar.copy(dst, src)
-            cols = slice(n * HALF, (n + 1) * HALF)
-            quantize(w1_codes[:, cols], w1_scales[:, cols], grouped[:])
+        grouped = deal(nc.vector.tensor_copy, w1_raw, 1, "w1_odd", "w1g_w2raw")
+        quantize(w1_codes[:, :HALF], w1_scales[:, :HALF], grouped[:])
+        grouped = deal(nc.scalar.copy, w1_raw, 0, "w1_even", "w1_even")
+        quantize(w1_codes[:, HALF:], w1_scales[:, HALF:], grouped[:])
 
-        w2_raw = keep.tile([P, PACK, S], F32, name="w2_raw", tag="raw")
-        nc.sync.dma_start(w2_raw[:], w2.rearrange("(p j) c -> p j c", j=PACK))
-        w3_raw = keep.tile([P, PACK, S], F32, name="w3_raw", tag="w1g_w3raw", align_bytes=64)
+        w3_raw = keep.tile([P, PACK, S], F32, name="w3_raw", tag="raw")
         nc.sync.dma_start(w3_raw[:], w3.rearrange("(p j) c -> p j c", j=PACK))
+        w2_raw = keep.tile([P, PACK, S], F32, name="w2_raw", tag="w1g_w2raw", align_bytes=64)
+        nc.sync.dma_start(w2_raw[:], w2.rearrange("(p j) c -> p j c", j=PACK))
 
         x_codes = keep.tile([P, S], U32, name="x_codes", align_bytes=64)
         for h in range(2):
@@ -119,42 +118,38 @@ def tile_picked_crossfft_none_p_kernel(
             nb[t] = keep.tile([P, V], F32, name="nb%d" % t)
             nc.vector.tensor_copy(a[t][:], y[t][:].indirect(la_t[:]))
             nc.vector.tensor_copy(b[t][:], y[t][:].indirect(lb_t[:]))
-            nc.scalar.activation(nb[t][:], b[t][:], COPY, scale=-1.0)
-
-        w2_grouped = keep.tile([P, PACK * S], BF16, name="w2_grouped", align_bytes=64)
-        for h in range(2):
-            dst, src = dealt_views(w2_grouped, w2_raw, h * 64, (h + 1) * 64)
-            nc.scalar.copy(dst, src)
-        res_t = keep.tile([P, PACK, S], F32, name="res_t", tag="raw")
-        nc.sync.dma_start(res_t[:], res.rearrange("(t p) j -> p t j", p=P))
-
-        def scatter_pair(window, planes):
-            for t in planes:
-                nc.vector.tensor_tensor(window[t][:].indirect(la_t[:]), a[t][:], b[t][:], ADD)
-            for t in planes:
-                nc.vector.tensor_tensor(window[t][:].indirect(lb_t[:]), a[t][:], nb[t][:], ADD)
-
-        z_odd = {
-            1: windows.tile([P, S], F32, name="z1", offset=5 * row_bytes // 2),
-            3: windows.tile([P, S], F32, name="z3", offset=7 * row_bytes // 2),
-        }
-        scatter_pair(z_odd, (1, 3))
-        z_pair = {}
-        for t in (0, 2):
-            z_pair[t] = keep.tile([P, 2 * S], F32, name="z_pair%d" % t)
-            nc.scalar.copy(z_pair[t][:, S:], z_odd[t + 1][:])
-
-        w2_codes = keep.tile([P, S], U32, name="w2_codes", align_bytes=64)
-        w2_scales = keep.tile([P, S], U8, name="w2_scales", align_bytes=64)
-        quantize(w2_codes[:], w2_scales[:], w2_grouped[:])
+            if t % 2:
+                nc.scalar.activation(nb[t][:], b[t][:], COPY, scale=-1.0)
 
         w3_grouped = keep.tile([P, PACK * S], BF16, name="w3_grouped", align_bytes=64)
         nc.scalar.copy(
             w3_grouped[:].rearrange("p (c i j) -> p c j i", i=4, j=PACK),
             w3_raw[:].rearrange("p j (c i) -> p c j i", i=4),
         )
+        res_t = keep.tile([P, PACK, S], F32, name="res_t", tag="raw")
+        nc.sync.dma_start(res_t[:], res.rearrange("(t p) j -> p t j", p=P))
 
-        scatter_pair(z_pair, (0, 2))
+        z_odd = {
+            1: windows.tile([P, S], F32, name="z1", offset=5 * row_bytes // 2),
+            3: windows.tile([P, S], F32, name="z3", offset=7 * row_bytes // 2),
+        }
+        for t in (1, 3):
+            nc.vector.tensor_tensor(z_odd[t][:].indirect(la_t[:]), a[t][:], b[t][:], ADD)
+        for t in (1, 3):
+            nc.vector.tensor_tensor(z_odd[t][:].indirect(lb_t[:]), a[t][:], nb[t][:], ADD)
+
+        w2_codes = keep.tile([P, S], U32, name="w2_codes", align_bytes=64)
+        w2_scales = keep.tile([P, S], U8, name="w2_scales", align_bytes=64)
+        z_pair = {}
+        for n, t in enumerate((0, 2)):
+            z_pair[t] = keep.tile([P, 2 * S], F32, name="z_pair%d" % t)
+            nc.scalar.copy(z_pair[t][:, S:], z_odd[t + 1][:])
+            nc.vector.tensor_tensor(z_pair[t][:].indirect(la_t[:]), a[t][:], b[t][:], ADD)
+            grouped = deal(nc.scalar.copy, w2_raw, n, "w2_grouped%d" % n, "w2_grouped%d" % n)
+            cols = slice(n * HALF, (n + 1) * HALF)
+            quantize(w2_codes[:, cols], w2_scales[:, cols], grouped[:])
+            nc.scalar.activation(nb[t][:], b[t][:], COPY, scale=-1.0)
+            nc.vector.tensor_tensor(z_pair[t][:].indirect(lb_t[:]), a[t][:], nb[t][:], ADD)
 
         z_grouped = [
             keep.tile([P, HALF, PACK], BF16, name="z_grouped%d" % h, tag="zg%d" % h, align_bytes=64) for h in range(2)
@@ -169,20 +164,18 @@ def tile_picked_crossfft_none_p_kernel(
         for h in range(2):
             dst, src = pair_views(0, h * HALF, (h + 1) * HALF)
             nc.scalar.copy(dst, src)
-        for c0, c1 in ((0, HALF), (HALF, HALF + CHUNK)):
-            dst, src = pair_views(2, c0, c1)
-            nc.vector.tensor_copy(dst, src)
-        dst, src = pair_views(2, HALF + CHUNK, S)
-        nc.scalar.copy(dst, src)
+        for c0 in range(0, S, CHUNK):
+            dst, src = pair_views(2, c0, c0 + CHUNK)
+            (nc.vector.tensor_copy if c0 < HALF else nc.scalar.copy)(dst, src)
 
         z_codes = keep.tile([P, S], U32, name="z_codes", align_bytes=64)
         z_scales = keep.tile([P, S], U8, name="z_scales", align_bytes=64)
-        z_pieces = ((0, HALF), (HALF, HALF + CHUNK), (HALF + CHUNK, S))
+        z_pieces = ((0, CHUNK), (CHUNK, HALF), (HALF, S))
         for c0, c1 in z_pieces:
             h = c0 // HALF
             grouped = z_grouped[h][:, c0 - h * HALF : c1 - h * HALF, :].rearrange("p c t -> p (c t)")
             quantize(z_codes[:, c0:c1], z_scales[:, c0:c1], grouped)
-        w3_codes = keep.tile([P, S], U32, name="w3_codes", tag="zg0", align_bytes=64)
+        w3_codes = keep.tile([P, S], U32, name="w3_codes", tag="zg1", align_bytes=64)
         w3_scales = keep.tile([P, S], U8, name="w3_scales", align_bytes=64)
         quantize(w3_codes[:], w3_scales[:], w3_grouped[:])
 
@@ -197,14 +190,14 @@ def tile_picked_crossfft_none_p_kernel(
             )
 
         first = []
-        for c0, c1 in z_pieces:
+        for c0, c1 in ((0, HALF), (HALF, S)):
             cols = slice(c0, c1)
             acc = psum.tile([P, c1 - c0], F32, name="acc", tag="bank")
             product(acc[:], w2_codes, w2_scales, 0, z_codes[:, cols], z_scales[:, cols])
             nc.scalar.activation(neg_h[0][:, cols], acc[:], COPY, scale=-1.0)
             first.append((cols, acc))
         for n, (cols, acc) in enumerate(first):
-            if n < 2:
+            if n == 0:
                 nc.vector.tensor_copy(h_plain[:, 0, cols], acc[:])
             else:
                 nc.scalar.copy(h_plain[:, 0, cols], acc[:])
@@ -213,7 +206,7 @@ def tile_picked_crossfft_none_p_kernel(
         h_acc = {}
         for t in range(1, PACK):
             h_acc[t] = psum.tile([P, S], F32, name="acc", tag="bank")
-            product(h_acc[t][:], w2_codes, w2_scales, t, z_codes[:], z_scales[:])
+            product(h_acc[t][:], w2_codes, w2_scales, (0, 2, 1, 3)[t], z_codes[:], z_scales[:])
             nc.scalar.activation(neg_h[t][:], h_acc[t][:], COPY, scale=-1.0)
             if t == 1:
                 nc.scalar.copy(h_plain[:, 1, :], h_acc[1][:])

from contextlib import ExitStack

import concourse.mybir as mybir

F32 = mybir.dt.float32
BF16 = mybir.dt.bfloat16
I32 = mybir.dt.int32
U32 = mybir.dt.uint32
U16 = mybir.dt.uint16
U8 = mybir.dt.uint8
FP8X4 = mybir.dt.float8_e4m3fn_x4
ADD = mybir.AluOpType.add
MULT = mybir.AluOpType.mult
COPY = mybir.ActivationFunctionType.Copy

P = 128
PACK = 4
T = 2048
S = 512
V = 256
HALF = 256
CHUNK = 128
FLOPS = 3 * 2 * 512 * 512 * 512


def tile_picked_crossfft_none_p_kernel(
    tc, x_words, x_scales, w1, w2, res, w3, offs, la, lb, mate, out
):
    nc = tc.nc
    with ExitStack() as ctx:
        lists = ctx.enter_context(tc.tile_pool(name="lists", bufs=1))
        keep = ctx.enter_context(tc.tile_pool(name="keep", bufs=1))
        windows = ctx.enter_context(tc.tile_pool(name="windows", bufs=1))
        psum = ctx.enter_context(tc.psum_pool(name="psum", bufs=8))

        def entries(tile, first, count):
            return tile[:, first // 16 : (first + count) // 16]

        def quantize(codes, scales, grouped):
            nc.vector.quantize_mx(out=codes.bitcast(FP8X4), scales=scales, in_=grouped)

        def product(acc, w_codes, w_scales, t, codes, scales):
            cols = slice(t * P, (t + 1) * P)
            nc.tensor.matmul_mx(
                out=acc, lhsT=w_codes[:, cols].bitcast(FP8X4), lhsT_scale=w_scales[:, cols],
                rhs=codes.bitcast(FP8X4), rhs_scale=scales, start=True, stop=True,
            )

        def dealt_views(grouped, raw, m0, m1):
            dst = grouped[:].rearrange("p (t m j) -> p m j t", t=PACK, j=PACK)[:, m0:m1]
            src = raw[:].rearrange("p j (m t) -> p m j t", t=PACK)[:, m0:m1]
            return dst, src

        xs_table = keep.tile([P, T], U8, name="xs_table")
        nc.vector.memset(xs_table[:].bitcast(I32), 0)
        offs_t = lists.tile([P, S // 16], U16, name="offs_t")
        nc.sync.dma_start(offs_t[:], offs)
        xs_rows = keep.tile([P, T], U8, name="xs_rows")
        for q in range(4):
            rows = slice(32 * q, 32 * q + 4)
            (nc.scalar if q < 2 else nc.sync).dma_start(xs_rows[rows, :].bitcast(I32), x_scales[0, 4 * q : 4 * q + 4, :].bitcast(I32))
            nc.vector.tensor_copy(xs_table[rows, :].bitcast(I32), xs_rows[rows, :].bitcast(I32))
        w1_raw = keep.tile([P, PACK, S], F32, name="w1_raw", tag="raw")
        nc.sync.dma_start(w1_raw[:], w1.rearrange("(p j) c -> p j c", j=PACK))
        xw_table = keep.tile([P, T], U32, name="xw_table")
        nc.sync.dma_start(xw_table[:].bitcast(I32), x_words[0].rearrange("p n t -> p (n t)").bitcast(I32))
        la_t = lists.tile([P, V // 16], U16, name="la_t")
        nc.sync.dma_start(la_t[:], la)
        lb_t = lists.tile([P, V // 16], U16, name="lb_t")
        nc.sync.dma_start(lb_t[:], lb)
        mate_t = lists.tile([P, S // 16], U16, name="mate_t")
        nc.sync.dma_start(mate_t[:], mate)

        x_sc = keep.tile([P, S], U8, name="x_sc", align_bytes=64)
        nc.vector.tensor_copy(x_sc[:], xs_table[:].indirect(offs_t[:]))

        def deal(engine_copy, raw, odd, name, tag):
            grouped = keep.tile([P, 2 * P * PACK], BF16, name=name, tag=tag, align_bytes=64)
            dst = grouped[:].rearrange("p (u m j) -> p m j u", u=2, j=PACK)
            src = raw[:].rearrange("p j (m u v) -> p m j u v", u=2, v=2)[:, :, :, :, odd]
            engine_copy(dst, src)
            return grouped

        w1_codes = keep.tile([P, S], U32, name="w1_codes", align_bytes=64)
        w1_scales = keep.tile([P, S], U8, name="w1_scales", align_bytes=64)
        grouped = deal(nc.vector.tensor_copy, w1_raw, 1, "w1_odd", "w1g_w2raw")
        quantize(w1_codes[:, :HALF], w1_scales[:, :HALF], grouped[:])
        grouped = deal(nc.scalar.copy, w1_raw, 0, "w1_even", "w1_even")
        quantize(w1_codes[:, HALF:], w1_scales[:, HALF:], grouped[:])

        w3_raw = keep.tile([P, PACK, S], F32, name="w3_raw", tag="raw")
        nc.sync.dma_start(w3_raw[:], w3.rearrange("(p j) c -> p j c", j=PACK))
        w2_raw = keep.tile([P, PACK, S], F32, name="w2_raw", tag="w1g_w2raw", align_bytes=64)
        nc.sync.dma_start(w2_raw[:], w2.rearrange("(p j) c -> p j c", j=PACK))

        x_codes = keep.tile([P, S], U32, name="x_codes", align_bytes=64)
        for h in range(2):
            cols = slice(h * HALF, (h + 1) * HALF)
            nc.vector.tensor_copy(x_codes[:, cols], xw_table[:].indirect(entries(offs_t, h * HALF, HALF)))

        order = (1, 3, 0, 2)
        row_bytes = S * 4
        y = {}
        for n, t in enumerate(order):
            y[t] = windows.tile([P, S], F32, name="y%d" % t, offset=n * row_bytes)
            pieces = 2 if n == 0 else 1
            width = S // pieces
            for h in range(pieces):
                cols = slice(h * width, (h + 1) * width)
                acc = psum.tile([P, width], F32, name="acc", tag="bank")
                product(acc[:], w1_codes, w1_scales, n, x_codes[:, cols], x_sc[:, cols])
                nc.scalar.copy(y[t][:, cols], acc[:])

        a, b, nb = {}, {}, {}
        for t in order:
            a[t] = keep.tile([P, V], F32, name="a%d" % t)
            b[t] = keep.tile([P, V], F32, name="b%d" % t)
            nb[t] = keep.tile([P, V], F32, name="nb%d" % t)
            nc.vector.tensor_copy(a[t][:], y[t][:].indirect(la_t[:]))
            nc.vector.tensor_copy(b[t][:], y[t][:].indirect(lb_t[:]))
            if t % 2:
                nc.scalar.activation(nb[t][:], b[t][:], COPY, scale=-1.0)

        w3_grouped = keep.tile([P, PACK * S], BF16, name="w3_grouped", align_bytes=64)
        nc.scalar.copy(
            w3_grouped[:].rearrange("p (c i j) -> p c j i", i=4, j=PACK),
            w3_raw[:].rearrange("p j (c i) -> p c j i", i=4),
        )
        res_t = keep.tile([P, PACK, S], F32, name="res_t", tag="raw")
        nc.sync.dma_start(res_t[:], res.rearrange("(t p) j -> p t j", p=P))

        z_odd = {
            1: windows.tile([P, S], F32, name="z1", offset=5 * row_bytes // 2),
            3: windows.tile([P, S], F32, name="z3", offset=7 * row_bytes // 2),
        }
        for t in (1, 3):
            nc.vector.tensor_tensor(z_odd[t][:].indirect(la_t[:]), a[t][:], b[t][:], ADD)
        for t in (1, 3):
            nc.vector.tensor_tensor(z_odd[t][:].indirect(lb_t[:]), a[t][:], nb[t][:], ADD)

        w2_codes = keep.tile([P, S], U32, name="w2_codes", align_bytes=64)
        w2_scales = keep.tile([P, S], U8, name="w2_scales", align_bytes=64)
        z_pair = {}
        for n, t in enumerate((0, 2)):
            z_pair[t] = keep.tile([P, 2 * S], F32, name="z_pair%d" % t)
            nc.scalar.copy(z_pair[t][:, S:], z_odd[t + 1][:])
            nc.vector.tensor_tensor(z_pair[t][:].indirect(la_t[:]), a[t][:], b[t][:], ADD)
            grouped = deal(nc.scalar.copy, w2_raw, n, "w2_grouped%d" % n, "w2_grouped%d" % n)
            cols = slice(n * HALF, (n + 1) * HALF)
            quantize(w2_codes[:, cols], w2_scales[:, cols], grouped[:])
            nc.scalar.activation(nb[t][:], b[t][:], COPY, scale=-1.0)
            nc.vector.tensor_tensor(z_pair[t][:].indirect(lb_t[:]), a[t][:], nb[t][:], ADD)

        z_grouped = [
            keep.tile([P, HALF, PACK], BF16, name="z_grouped%d" % h, tag="zg%d" % h, align_bytes=64) for h in range(2)
        ]

        def pair_views(t, c0, c1):
            h = c0 // HALF
            dst = z_grouped[h][:, c0 - h * HALF : c1 - h * HALF, t : t + 2]
            src = z_pair[t][:].rearrange("p (s j) -> p j s", s=2)[:, c0:c1, :]
            return dst, src

        for h in range(2):
            dst, src = pair_views(0, h * HALF, (h + 1) * HALF)
            nc.scalar.copy(dst, src)
        for c0 in range(0, S, CHUNK):
            dst, src = pair_views(2, c0, c0 + CHUNK)
            (nc.vector.tensor_copy if c0 < HALF else nc.scalar.copy)(dst, src)

        z_codes = keep.tile([P, S], U32, name="z_codes", align_bytes=64)
        z_scales = keep.tile([P, S], U8, name="z_scales", align_bytes=64)
        z_pieces = ((0, CHUNK), (CHUNK, HALF), (HALF, S))
        for c0, c1 in z_pieces:
            h = c0 // HALF
            grouped = z_grouped[h][:, c0 - h * HALF : c1 - h * HALF, :].rearrange("p c t -> p (c t)")
            quantize(z_codes[:, c0:c1], z_scales[:, c0:c1], grouped)
        w3_codes = keep.tile([P, S], U32, name="w3_codes", tag="zg1", align_bytes=64)
        w3_scales = keep.tile([P, S], U8, name="w3_scales", align_bytes=64)
        quantize(w3_codes[:], w3_scales[:], w3_grouped[:])

        neg_h = [keep.tile([P, S], F32, name="neg_h%d" % t, tag="neg_h%d" % t, align_bytes=64) for t in range(PACK)]
        h_plain = keep.tile([P, PACK, S], F32, name="h_plain")
        z2 = keep.tile([P, PACK, S], F32, name="z2")

        def subtract_mate(t, c0, width):
            cols = slice(c0, c0 + width)
            nc.vector.tensor_tensor(
                z2[:, t, cols], neg_h[t][:].indirect(entries(mate_t, c0, width)), h_plain[:, t, cols], ADD
            )

        first = []
        for c0, c1 in ((0, HALF), (HALF, S)):
            cols = slice(c0, c1)
            acc = psum.tile([P, c1 - c0], F32, name="acc", tag="bank")
            product(acc[:], w2_codes, w2_scales, 0, z_codes[:, cols], z_scales[:, cols])
            nc.scalar.activation(neg_h[0][:, cols], acc[:], COPY, scale=-1.0)
            first.append((cols, acc))
        for n, (cols, acc) in enumerate(first):
            if n == 0:
                nc.vector.tensor_copy(h_plain[:, 0, cols], acc[:])
            else:
                nc.scalar.copy(h_plain[:, 0, cols], acc[:])
        for h in range(2):
            subtract_mate(0, h * HALF, HALF)
        h_acc = {}
        for t in range(1, PACK):
            h_acc[t] = psum.tile([P, S], F32, name="acc", tag="bank")
            product(h_acc[t][:], w2_codes, w2_scales, (0, 2, 1, 3)[t], z_codes[:], z_scales[:])
            nc.scalar.activation(neg_h[t][:], h_acc[t][:], COPY, scale=-1.0)
            if t == 1:
                nc.scalar.copy(h_plain[:, 1, :], h_acc[1][:])
                for h in range(2):
                    subtract_mate(1, h * HALF, HALF)
            else:
                nc.scalar.copy(h_plain[:, t, :HALF], h_acc[t][:, :HALF])
                subtract_mate(t, 0, HALF)
        for t in (2, 3):
            nc.scalar.copy(h_plain[:, t, HALF:], h_acc[t][:, HALF:])
        subtract_mate(2, HALF, HALF)
        for c0 in (HALF, HALF + CHUNK):
            subtract_mate(3, c0, CHUNK)

        out_view = out.rearrange("(t p) j -> p t j", p=P)
        finals = []
        for c in range(S // CHUNK):
            cols = slice(c * CHUNK, (c + 1) * CHUNK)
            z2_grouped = keep.tile([P, CHUNK * PACK], BF16, name="z2_grouped", tag="z2_grouped%d" % c, align_bytes=64)
            nc.scalar.copy(
                z2_grouped[:].rearrange("p (c i t) -> p c t i", i=4, t=PACK),
                z2[:, :, cols].rearrange("p t (c i) -> p c t i", i=4),
            )
            z2_codes = keep.tile([P, CHUNK], U32, name="z2_codes%d" % c, align_bytes=64)
            z2_scales = keep.tile([P, CHUNK], U8, name="z2_scales%d" % c, align_bytes=64)
            quantize(z2_codes[:], z2_scales[:], z2_grouped[:])
            pieces = 2 if c == S // CHUNK - 1 else 1
            rows = PACK // pieces
            for n in range(pieces):
                acc = psum.tile([P, rows, CHUNK], F32, name="acc", tag="bank")
                for t in range(rows):
                    product(acc[:, t, :], w3_codes, w3_scales, n * rows + t, z2_codes[:], z2_scales[:])
                finals.append((acc, slice(n * rows, (n + 1) * rows), cols))
        for n, (acc, rows, cols) in enumerate(finals):
            tag = ("neg_h2", "neg_h3", "z2_grouped3", "neg_h0", "neg_h1")[n]
            result = keep.tile([P, rows.stop - rows.start, CHUNK], F32, name="result", tag=tag, align_bytes=64)
            nc.vector.scalar_tensor_tensor(result[:], acc[:], 0.5, res_t[:, rows, cols], MULT, ADD)
            (nc.scalar if n == len(finals) - 1 else nc.sync).dma_start(out_view[:, rows, cols], result[:])
